import numpy as np
import ml_dtypes


def mxq(x, axis, fmt="e4m3"):
    dtype, down = {"e4m3": (ml_dtypes.float8_e4m3fn, 7), "e5m2": (ml_dtypes.float8_e5m2, 14)}[fmt]
    v = np.moveaxis(np.asarray(x, np.float32).astype(ml_dtypes.bfloat16).astype(np.float64), axis, -1)
    blocks = v.reshape(v.shape[:-1] + (-1, 32))
    amax = np.abs(blocks).max(-1, keepdims=True)
    byte = np.maximum(np.where(amax > 0, np.frexp(amax)[1] - 1 + 127, 0) - down, 1)
    scale = np.exp2(byte - 127.0)
    codes = (blocks / scale).astype(np.float32).astype(dtype).astype(np.float64)
    return np.moveaxis((codes * scale).reshape(v.shape), -1, axis)


WIDE = False


def mx_kscale(k):
    if not WIDE:
        return np.ones(k)
    levels = np.array([10, -10, 5, -5, 0])
    if k % 512:
        return np.exp2(np.random.permutation(np.resize(levels, k // 32))).repeat(32)
    a = np.empty((k // 512, 16))
    for p in range(k // 512):
        a[p, :8] = np.random.permutation(np.resize(levels, 8))
        for g in range(8):
            far = levels[np.abs(levels - a[p, g]) >= 10]
            a[p, g + 8] = far[np.random.randint(len(far))]
    return np.exp2(a.ravel()).repeat(32)


def f64(x):
    return np.asarray(x).astype(np.float64)


def striped(idx):
    return np.tile(idx.reshape(-1, 16).T, (8, 1)).astype(np.uint16)


def unstriped(offs):
    return offs[:16].T.reshape(-1).astype(np.int64)


def pack_weight(w):
    k, n = w.shape
    w = f64(np.asarray(w, np.float32).astype(ml_dtypes.bfloat16)).reshape(k // 32, 32, n)
    amax = np.abs(w).max(1)
    byte = np.clip(np.where(amax > 0, np.frexp(amax)[1] - 1 + 127 - 7, 1), 1, 254)
    scaled = (w * np.exp2(127.0 - byte)[:, None, :]).reshape(k, n).astype(np.float32)
    words = np.ascontiguousarray(scaled.reshape(k // 512, 128, 4, n).transpose(0, 1, 3, 2)).astype(ml_dtypes.float8_e4m3fn).view(np.uint8)
    return words, np.ascontiguousarray(byte.astype(np.uint8).reshape(k // 512, 16, n))


def unpack_weight(words, scales):
    g, p, n, _ = words.shape
    vals = np.ascontiguousarray(words).view(ml_dtypes.float8_e4m3fn).astype(np.float64) * np.repeat(np.exp2(scales.astype(np.float64) - 127.0), 8, axis=1)[..., None]
    return vals.transpose(0, 1, 3, 2).reshape(g * 512, n)


def planes(y):
    n, m = y.shape
    v = y.astype(np.float32).astype(ml_dtypes.bfloat16).astype(np.float64).reshape(n // 32, 32, m)
    top = np.abs(v).max(1)
    byte = np.clip(np.where(top > 0, np.frexp(top)[1] - 1 + 127 - 7, 1), 1, 254)
    codes = (v * np.exp2(127.0 - byte)[:, None, :]).reshape(n, m).astype(np.float32).astype(ml_dtypes.float8_e4m3fn).view(np.uint8)
    words = codes.reshape(n // 512, 128, 4, m).transpose(0, 1, 3, 2)
    return np.ascontiguousarray(words), np.ascontiguousarray(byte.astype(np.uint8).reshape(n // 512, 16, m))


K, T, S, N, U = 1024, 4096, 1024, 512, 2048


def setup_inputs():
    n = np.random.standard_normal
    s = mx_kscale(K)[:, None]
    packed_xT = pack_weight(n((K, T)) * s)
    return {
        "x_words": packed_xT[0],
        "x_scales": packed_xT[1],
        "state": (n((N, U))).astype(np.float32),
        "w1": (n((K, N)) / np.sqrt(K) / s).astype(np.float32),
        "w2": (n((K, N)) / np.sqrt(K) / s).astype(np.float32),
        "bias": (-np.random.uniform(0.5, 2.0, (N, 1))).astype(np.float32),
        "rate": (-np.random.uniform(0.3, 2.0, (N, 1))).astype(np.float32),
        "offs": striped(np.random.permutation(T)[:S]),
        "slot": striped(np.random.permutation(U)[:S]),
    }


def reference(x_words, x_scales, state, w1, w2, bias, rate, offs, slot):
    old = f64(state)[:, unstriped(slot)]
    xq = unpack_weight(x_words, x_scales)[:, unstriped(offs)]
    dt = np.log(np.exp((mxq(f64(w1), 0, "e4m3").T @ xq) + f64(bias)) + 1.0)
    a = np.exp(f64(rate) * dt)
    y = mxq(f64(w2), 0, "e4m3").T @ xq
    new = old * a + dt * y
    out = f64(state).copy()
    out[:, unstriped(slot)] = new
    out_0 = out
    return (out_0,) + planes(out_0)

@@ -1,0 +1,292 @@
+from contextlib import ExitStack
+
+import concourse.mybir as mybir
+from concourse.masks import make_identity
+
+K, T, S, N, U = 1024, 4096, 1024, 512, 2048
+FLOPS = 2 * 2 * K * S * N
+
+F32 = mybir.dt.float32
+BF16 = mybir.dt.bfloat16
+I32 = mybir.dt.int32
+U32 = mybir.dt.uint32
+U16 = mybir.dt.uint16
+U8 = mybir.dt.uint8
+FP8X4 = mybir.dt.float8_e4m3fn_x4
+ALU = mybir.AluOpType
+ACT = mybir.ActivationFunctionType
+
+P = 128
+PASSES = K // 512
+BLOCKS = N // P
+HALF = 512
+HALVES = S // HALF
+LIST_COLS = HALF // 16
+QUARTER = U // 4
+CLAMP = 32.0
+W_PIECES = ((0, 1), (1, 1), (2, 2))
+
+
+def tile_picked_ymamba_step_po_kernel(
+    tc, x_words, x_scales, state, w1, w2, bias, rate, offs, slot, out_0, out_1, out_2
+):
+    nc = tc.nc
+    with ExitStack() as ctx:
+        keep = ctx.enter_context(tc.tile_pool(name="keep", bufs=1))
+        work = ctx.enter_context(tc.tile_pool(name="work", bufs=2))
+        psum = ctx.enter_context(tc.psum_pool(name="psum", bufs=2))
+
+        offs_t = keep.tile([P, S // 16], U16, name="offs_t")
+        slot_t = keep.tile([P, S // 16], U16, name="slot_t")
+        x_table = [keep.tile([P, T], I32, name=f"x_table{g}") for g in range(PASSES)]
+        scale_table = keep.tile([P, T], U8, name="scale_table", tag="scales_then_codes", align_bytes=64)
+        x_picked = [keep.tile([P, S], I32, name="x_picked0", align_bytes=64)]
+        x_plane = keep.tile([P, S], U8, name="x_plane", align_bytes=64)
+        states = [keep.tile([P, U], F32, name=f"states{b}") for b in range(BLOCKS)]
+        w_raw = {}
+        for i in range(2):
+            for first, count in W_PIECES:
+                tile = keep.tile([P, PASSES, 4, count * P], F32, name=f"w_raw{i}_{first}")
+                for b in range(first, first + count):
+                    w_raw[i, b] = (tile, b - first)
+        bias_t = keep.tile([P, BLOCKS], F32, name="bias_t")
+        rate_t = keep.tile([P, BLOCKS], F32, name="rate_t")
+        room_t = keep.tile([P, BLOCKS], F32, name="room_t")
+        ident = keep.tile([P, P], F32, name="ident")
+        out_plane = keep.tile([P, QUARTER], U8, name="out_plane", align_bytes=64)
+        weights = (w1, w2)
+
+        def load_x(g):
+            nc.sync.dma_start(x_table[g][:], x_words[g].rearrange("p n t -> p (n t)").bitcast(I32))
+
+        def load_w(i, piece):
+            first, count = W_PIECES[piece]
+            for g in range(PASSES):
+                rows = weights[i][g * 512 : (g + 1) * 512, first * P : (first + count) * P]
+                nc.sync.dma_start(w_raw[i, first][0][:, g], rows.rearrange("(p j) c -> p j c", j=4))
+
+        def load_state(b):
+            nc.sync.dma_start(states[b][:], state[b * P : (b + 1) * P, :])
+
+        nc.gpsimd.memset(scale_table[:].bitcast(I32), 0)
+        for g in range(PASSES):
+            for r in range(4):
+                queue = nc.gpsimd if 4 * g + r < 3 else nc.scalar
+                queue.dma_start(scale_table[4 * g + r : P : 32, :].bitcast(I32), x_scales[g, r:16:4, :].bitcast(I32))
+        nc.sync.dma_start(offs_t[:], offs)
+        nc.sync.dma_start(slot_t[:], slot)
+        with nc.allow_non_contiguous_dma(reason="one value a partition"):
+            nc.scalar.dma_start(bias_t[:], bias.rearrange("(b p) o -> p (b o)", p=P))
+            nc.scalar.dma_start(rate_t[:], rate.rearrange("(b p) o -> p (b o)", p=P))
+        load_x(0)
+        load_w(0, 0)
+        load_x(1)
+        load_w(0, 1)
+        load_w(1, 0)
+        load_state(0)
+        load_w(1, 1)
+        load_w(0, 2)
+        load_state(1)
+        load_w(1, 2)
+        load_state(2)
+        load_state(3)
+        make_identity(nc, ident[:])
+
+        nc.vector.tensor_scalar(room_t[:], bias_t[:], -1.0, CLAMP, ALU.mult, ALU.add)
+
+        def pick_x(g, h):
+            nc.vector.tensor_copy(
+                x_picked[g][:, h * HALF : (h + 1) * HALF].bitcast(U32),
+                x_table[g][:].bitcast(U32).indirect(offs_t[:, h * LIST_COLS : (h + 1) * LIST_COLS]),
+            )
+
+        w_codes = {}
+
+        def quantize_w(i, b, engine, tag="grouped"):
+            tile, place = w_raw[i, b]
+            raw = tile[:, :, :, place * P : (place + 1) * P]
+            pool = work if tag == "grouped" else keep
+            grouped = pool.tile([P, PASSES, P, 4], BF16, name="grouped", tag=tag, align_bytes=64)
+            if engine == "scalar":
+                nc.scalar.copy(grouped[:], raw.rearrange("p g j c -> p g c j"))
+            else:
+                nc.vector.tensor_copy(grouped[:], raw.rearrange("p g j c -> p g c j"))
+            codes = keep.tile([P, PASSES * P], I32, name=f"w_codes{i}_{b}", align_bytes=64)
+            plane = keep.tile([P, PASSES * P], U8, name=f"w_plane{i}_{b}", align_bytes=64)
+            nc.vector.quantize_mx(codes[:].bitcast(FP8X4), plane[:], grouped[:].rearrange("p g c j -> p (g c j)"))
+            w_codes[i, b] = (codes, plane)
+
+        def product(i, b, h, name):
+            codes, plane = w_codes[i, b]
+            acc = psum.tile([P, HALF], F32, name=name)
+            cols = slice(h * HALF, (h + 1) * HALF)
+            for g in range(PASSES):
+                nc.tensor.matmul_mx(
+                    acc[:],
+                    lhsT=codes[:, g * P : (g + 1) * P].bitcast(FP8X4),
+                    lhsT_scale=plane[:, g * P : (g + 1) * P],
+                    rhs=x_picked[g][:, cols].bitcast(FP8X4),
+                    rhs_scale=x_plane[4 * g : P, cols],
+                    start=(g == 0),
+                    stop=(g == PASSES - 1),
+                )
+            return acc
+
+        held = {}
+
+        def step_exp(b):
+            below = work.tile([P, S], F32, name="below")
+            zs = []
+            for h in range(HALVES):
+                z = product(0, b, h, "z")
+                nc.scalar.activation(
+                    below[:, h * HALF : (h + 1) * HALF], z[:], ACT.Relu, bias=room_t[:, b : b + 1], scale=-1.0
+                )
+                zs.append(z)
+            grown = keep.tile([P, S], F32, name="grown", tag=f"chain{b % 2}")
+            nc.scalar.activation(grown[:], below[:], ACT.Exp, bias=CLAMP, scale=-1.0)
+            held[b] = (grown, zs)
+
+        dts = {}
+        decays = {}
+        entered = {}
+        kepts = {}
+
+        def step_log(b):
+            grown, zs = held[b]
+            dt = work.tile([P, S], F32, name="dt")
+            soft = keep.tile([P, S], F32, name="soft", tag="soft", align_bytes=64)
+            if b > 0:
+                nc.scalar.activation(soft[:], grown[:], ACT.Ln, bias=1.0)
+            for h in range(HALVES):
+                cols = slice(h * HALF, (h + 1) * HALF)
+                if b == 0:
+                    nc.scalar.activation(soft[:, cols], grown[:, cols], ACT.Ln, bias=1.0)
+                nc.vector.scalar_tensor_tensor(
+                    dt[:, cols], zs[h][:], bias_t[:, b : b + 1], soft[:, cols], ALU.add, ALU.max
+                )
+            dts[b] = dt
+
+        def step_decay(b):
+            decay = keep.tile([P, S], F32, name="decay", tag=f"chain{b % 2}")
+            width = HALF if b == 0 else S
+            for c0 in range(0, S, width):
+                cols = slice(c0, c0 + width)
+                nc.scalar.activation(decay[:, cols], dts[b][:, cols], ACT.Exp, scale=rate_t[:, b : b + 1])
+            decays[b] = decay
+
+        def enter(b, h):
+            y = product(1, b, h, "y")
+            tile = keep.tile([P, HALF], F32, name="entered", tag=("entered0" if h == 0 else "soft"), align_bytes=64)
+            nc.vector.tensor_tensor(tile[:], y[:], dts[b][:, h * HALF : (h + 1) * HALF], ALU.mult)
+            entered[b, h] = tile
+
+        def keep_old(b):
+            kept = work.tile([P, S], F32, name="kept")
+            if b == 0:
+                for h in range(HALVES):
+                    cols = slice(h * HALF, (h + 1) * HALF)
+                    nc.vector.tensor_tensor(kept[:, cols], old_first[:, cols], decays[b][:, cols], ALU.mult)
+            else:
+                nc.vector.tensor_tensor(kept[:], states[b][:].indirect(slot_t[:]), decays[b][:], ALU.mult)
+            kepts[b] = kept
+
+        def put(b, h):
+            nc.vector.tensor_tensor(
+                states[b][:].indirect(slot_t[:, h * LIST_COLS : (h + 1) * LIST_COLS]),
+                kepts[b][:, h * HALF : (h + 1) * HALF],
+                entered[b, h][:],
+                ALU.add,
+            )
+
+        def turn(b, j, tag):
+            turned = psum.tile([P, 4, P], F32, name="turned", tag=tag)
+            for h in range(4):
+                c0 = h * QUARTER + j * P
+                nc.tensor.transpose(turned[:, h, :], states[b][:, c0 : c0 + P], ident[:])
+            return turned[:].rearrange("p h (q u e) -> p u (h q) e", u=2, e=2)
+
+        def turn_back(rounded_pair):
+            back = psum.tile([P, 2, 2, P], F32, name="back")
+            for jj in range(2):
+                words = rounded_pair[jj].rearrange("p u w e -> p (u w e)").bitcast(F32)
+                for u in range(2):
+                    nc.tensor.transpose(back[:, jj, u, :], words[:, u * P : (u + 1) * P], ident[:])
+            return back[:].rearrange("p j u c -> p j c u")
+
+        def store_codes(b, codes, queues):
+            rows = out_1[0, 32 * b : 32 * (b + 1)].rearrange("q c r -> q (c r)").bitcast(I32)
+            for h in range(4):
+                queues[h % 2].dma_start(rows[:, h * QUARTER : (h + 1) * QUARTER], codes[32 * h : 32 * (h + 1), :])
+
+        def hand_on(b):
+            rounded = keep.tile([P, 4, 2, P, 2], BF16, name="rounded", tag=f"chain{b % 2}")
+            for j in range(4):
+                nc.scalar.copy(rounded[:, j], turn(b, j, "turned"))
+            regrouped = work.tile([P, 4, P, 2], F32, name="regrouped", align_bytes=64)
+            for pair in range(2):
+                back = turn_back([rounded[:, 2 * pair], rounded[:, 2 * pair + 1]])
+                nc.scalar.copy(regrouped[:, 2 * pair : 2 * pair + 2, :, :], back)
+            codes = work.tile([P, QUARTER], I32, name="out_codes", align_bytes=64)
+            nc.vector.quantize_mx(
+                codes[:].bitcast(FP8X4),
+                out_plane[4 * b : P, :],
+                regrouped[:].rearrange("p j c u -> p (j c u)").bitcast(BF16),
+            )
+            store_codes(b, codes, (nc.sync, nc.sync))
+
+        def hand_on_last(b):
+            copies = (nc.scalar.copy, nc.vector.tensor_copy)
+            rounded = []
+            for j in range(4):
+                piece = keep.tile([P, 2, P, 2], BF16, name=f"last_rounded{j}")
+                copies[j % 2](piece[:], turn(b, j, "turned" if j < 2 else "z"))
+                rounded.append(piece[:])
+            codes = work.tile([P, QUARTER], I32, name="out_codes", align_bytes=64)
+            for pair in range(2):
+                back = turn_back(rounded[2 * pair : 2 * pair + 2])
+                regrouped = keep.tile([P, 2, P, 2], F32, name=f"last_regrouped{pair}", align_bytes=64)
+                copies[pair](regrouped[:], back)
+                cols = slice(pair * 2 * P, (pair + 1) * 2 * P)
+                nc.vector.quantize_mx(
+                    codes[:, cols].bitcast(FP8X4),
+                    out_plane[4 * b : P, cols],
+                    regrouped[:].rearrange("p j c u -> p (j c u)").bitcast(BF16),
+                )
+            store_codes(b, codes, (nc.sync, nc.scalar))
+
+        pick_x(0, 0)
+        pick_x(0, 1)
+        quantize_w(0, 0, "scalar")
+        nc.vector.tensor_copy(x_plane[:], scale_table[:].indirect(offs_t[:]))
+        x_picked.append(keep.tile([P, S], I32, name="x_picked1", tag="scales_then_codes", align_bytes=64))
+        pick_x(1, 0)
+        pick_x(1, 1)
+        quantize_w(0, 1, "vector")
+        quantize_w(1, 0, "vector")
+        step_exp(0)
+        old_first = keep.tile([P, S], F32, name="old_first")
+        nc.vector.tensor_copy(old_first[:], states[0][:].indirect(slot_t[:]))
+        step_log(0)
+        for b in range(BLOCKS):
+            enter(b, 0)
+            step_decay(b)
+            keep_old(b)
+            put(b, 0)
+            if b + 1 < BLOCKS:
+                quantize_w(1, b + 1, "vector")
+                step_exp(b + 1)
+                step_log(b + 1)
+            if b + 2 < BLOCKS:
+                quantize_w(0, b + 2, "vector", tag="soft")
+            enter(b, 1)
+            put(b, 1)
+            nc.sync.dma_start(out_0[b * P : (b + 1) * P, :], states[b][:])
+            if b > 0:
+                hand_on(b - 1)
+        hand_on_last(BLOCKS - 1)
+        for h in range(4):
+            (nc.scalar, nc.sync)[h % 2].dma_start(
+                out_2[0, :, h * QUARTER : (h + 1) * QUARTER].bitcast(I32),
+                out_plane[32 * h : 32 * h + 16, :].bitcast(I32),
+            )

@@ -33,12 +33,17 @@ def tile_picked_ymamba_step_po_kernel(
     nc = tc.nc
     with ExitStack() as ctx:
         keep = ctx.enter_context(tc.tile_pool(name="keep", bufs=1))
+        reused = ctx.enter_context(tc.tile_pool(name="reused", bufs=1))
+        after_log = ctx.enter_context(tc.tile_pool(name="after_log", bufs=1))
         work = ctx.enter_context(tc.tile_pool(name="work", bufs=2))
         psum = ctx.enter_context(tc.psum_pool(name="psum", bufs=2))
 
         offs_t = keep.tile([P, S // 16], U16, name="offs_t")
         slot_t = keep.tile([P, S // 16], U16, name="slot_t")
-        x_table = [keep.tile([P, T], I32, name=f"x_table{g}") for g in range(PASSES)]
+        x_table = [
+            keep.tile([P, T], I32, name="x_table0"),
+            reused.tile([P, T], I32, name="x_table1", offset=0, align_bytes=64),
+        ]
         scale_table = keep.tile([P, T], U8, name="scale_table", tag="scales_then_codes", align_bytes=64)
         x_picked = [keep.tile([P, S], I32, name="x_picked0", align_bytes=64)]
         x_plane = keep.tile([P, S], U8, name="x_plane", align_bytes=64)
@@ -49,8 +54,10 @@ def tile_picked_ymamba_step_po_kernel(
                 tile = keep.tile([P, PASSES, 4, count * P], F32, name=f"w_raw{i}_{first}")
                 for b in range(first, first + count):
                     w_raw[i, b] = (tile, b - first)
-        bias_t = keep.tile([P, BLOCKS], F32, name="bias_t")
-        rate_t = keep.tile([P, BLOCKS], F32, name="rate_t")
+        channel_rows = keep.tile([P, P], F32, name="channel_rows")
+        channel_cols = keep.tile([P, 2 * BLOCKS], F32, name="channel_cols")
+        bias_t = channel_cols[:, 0:BLOCKS]
+        rate_t = channel_cols[:, BLOCKS : 2 * BLOCKS]
         room_t = keep.tile([P, BLOCKS], F32, name="room_t")
         ident = keep.tile([P, P], F32, name="ident")
         out_plane = keep.tile([P, QUARTER], U8, name="out_plane", align_bytes=64)
@@ -68,22 +75,23 @@ def tile_picked_ymamba_step_po_kernel(
         def load_state(b):
             nc.sync.dma_start(states[b][:], state[b * P : (b + 1) * P, :])
 
+        nc.vector.memset(channel_rows[:], 0.0)
+        nc.scalar.dma_start(channel_rows[0:BLOCKS, :], bias.rearrange("(b p) o -> b (p o)", p=P))
+        nc.scalar.dma_start(channel_rows[BLOCKS : 2 * BLOCKS, :], rate.rearrange("(b p) o -> b (p o)", p=P))
         nc.gpsimd.memset(scale_table[:].bitcast(I32), 0)
         for g in range(PASSES):
             for r in range(4):
-                queue = nc.gpsimd if 4 * g + r < 3 else nc.scalar
-                queue.dma_start(scale_table[4 * g + r : P : 32, :].bitcast(I32), x_scales[g, r:16:4, :].bitcast(I32))
+                nc.gpsimd.dma_start(
+                    scale_table[4 * g + r : P : 32, :].bitcast(I32), x_scales[g, r:16:4, :].bitcast(I32)
+                )
         nc.sync.dma_start(offs_t[:], offs)
         nc.sync.dma_start(slot_t[:], slot)
-        with nc.allow_non_contiguous_dma(reason="one value a partition"):
-            nc.scalar.dma_start(bias_t[:], bias.rearrange("(b p) o -> p (b o)", p=P))
-            nc.scalar.dma_start(rate_t[:], rate.rearrange("(b p) o -> p (b o)", p=P))
         load_x(0)
         load_w(0, 0)
         load_x(1)
-        load_w(0, 1)
-        load_w(1, 0)
         load_state(0)
+        load_w(1, 0)
+        load_w(0, 1)
         load_w(1, 1)
         load_w(0, 2)
         load_state(1)
@@ -92,7 +100,10 @@ def tile_picked_ymamba_step_po_kernel(
         load_state(3)
         make_identity(nc, ident[:])
 
-        nc.vector.tensor_scalar(room_t[:], bias_t[:], -1.0, CLAMP, ALU.mult, ALU.add)
+        channel_turned = psum.tile([P, P], F32, name="channel_turned", tag="turned")
+        nc.tensor.transpose(channel_turned[:], channel_rows[:], ident[:])
+        nc.scalar.copy(channel_cols[:], channel_turned[:, 0 : 2 * BLOCKS])
+        nc.scalar.activation(room_t[:], channel_turned[:, 0:BLOCKS], ACT.Copy, bias=CLAMP, scale=-1.0)
 
         def pick_x(g, h):
             nc.vector.tensor_copy(
@@ -101,16 +112,22 @@ def tile_picked_ymamba_step_po_kernel(
             )
 
         w_codes = {}
+        w_rounded = {}
+        grouped_shape = [P, PASSES, P, 4]
 
-        def quantize_w(i, b, engine, tag="grouped"):
+        def grouped_in(tag):
+            return keep.tile(grouped_shape, BF16, name="grouped", tag=tag, align_bytes=64)
+
+        def grouped_at(offset):
+            return reused.tile(grouped_shape, BF16, name=f"grouped_at{offset}", offset=offset, align_bytes=64)
+
+        def round_w(i, b, grouped, copy):
             tile, place = w_raw[i, b]
-            raw = tile[:, :, :, place * P : (place + 1) * P]
-            pool = work if tag == "grouped" else keep
-            grouped = pool.tile([P, PASSES, P, 4], BF16, name="grouped", tag=tag, align_bytes=64)
-            if engine == "scalar":
-                nc.scalar.copy(grouped[:], raw.rearrange("p g j c -> p g c j"))
-            else:
-                nc.vector.tensor_copy(grouped[:], raw.rearrange("p g j c -> p g c j"))
+            copy(grouped[:], tile[:, :, :, place * P : (place + 1) * P].rearrange("p g j c -> p g c j"))
+            w_rounded[i, b] = grouped
+
+        def quantize_w(i, b):
+            grouped = w_rounded[i, b]
             codes = keep.tile([P, PASSES * P], I32, name=f"w_codes{i}_{b}", align_bytes=64)
             plane = keep.tile([P, PASSES * P], U8, name=f"w_plane{i}_{b}", align_bytes=64)
             nc.vector.quantize_mx(codes[:].bitcast(FP8X4), plane[:], grouped[:].rearrange("p g c j -> p (g c j)"))
@@ -143,7 +160,7 @@ def tile_picked_ymamba_step_po_kernel(
                     below[:, h * HALF : (h + 1) * HALF], z[:], ACT.Relu, bias=room_t[:, b : b + 1], scale=-1.0
                 )
                 zs.append(z)
-            grown = keep.tile([P, S], F32, name="grown", tag=f"chain{b % 2}")
+            grown = keep.tile([P, S], F32, name="grown", tag="grown")
             nc.scalar.activation(grown[:], below[:], ACT.Exp, bias=CLAMP, scale=-1.0)
             held[b] = (grown, zs)
 
@@ -155,7 +172,7 @@ def tile_picked_ymamba_step_po_kernel(
         def step_log(b):
             grown, zs = held[b]
             dt = work.tile([P, S], F32, name="dt")
-            soft = keep.tile([P, S], F32, name="soft", tag="soft", align_bytes=64)
+            soft = after_log.tile([P, S], F32, name="soft", offset=0, align_bytes=64)
             if b > 0:
                 nc.scalar.activation(soft[:], grown[:], ACT.Ln, bias=1.0)
             for h in range(HALVES):
@@ -168,7 +185,7 @@ def tile_picked_ymamba_step_po_kernel(
             dts[b] = dt
 
         def step_decay(b):
-            decay = keep.tile([P, S], F32, name="decay", tag=f"chain{b % 2}")
+            decay = keep.tile([P, S], F32, name="decay", tag=f"decay{b % 2}", align_bytes=64)
             width = HALF if b == 0 else S
             for c0 in range(0, S, width):
                 cols = slice(c0, c0 + width)
@@ -177,7 +194,10 @@ def tile_picked_ymamba_step_po_kernel(
 
         def enter(b, h):
             y = product(1, b, h, "y")
-            tile = keep.tile([P, HALF], F32, name="entered", tag=("entered0" if h == 0 else "soft"), align_bytes=64)
+            if h == 0:
+                tile = keep.tile([P, HALF], F32, name="entered0", align_bytes=64)
+            else:
+                tile = after_log.tile([P, HALF], F32, name="entered1", offset=0, align_bytes=64)
             nc.vector.tensor_tensor(tile[:], y[:], dts[b][:, h * HALF : (h + 1) * HALF], ALU.mult)
             entered[b, h] = tile
 
@@ -220,7 +240,7 @@ def tile_picked_ymamba_step_po_kernel(
                 queues[h % 2].dma_start(rows[:, h * QUARTER : (h + 1) * QUARTER], codes[32 * h : 32 * (h + 1), :])
 
         def hand_on(b):
-            rounded = keep.tile([P, 4, 2, P, 2], BF16, name="rounded", tag=f"chain{b % 2}")
+            rounded = keep.tile([P, 4, 2, P, 2], BF16, name="rounded", tag="grown")
             for j in range(4):
                 nc.scalar.copy(rounded[:, j], turn(b, j, "turned"))
             regrouped = work.tile([P, 4, P, 2], F32, name="regrouped", align_bytes=64)
@@ -257,29 +277,39 @@ def tile_picked_ymamba_step_po_kernel(
 
         pick_x(0, 0)
         pick_x(0, 1)
-        quantize_w(0, 0, "scalar")
+        round_w(0, 0, grouped_in("grouped"), nc.scalar.copy)
+        quantize_w(0, 0)
         nc.vector.tensor_copy(x_plane[:], scale_table[:].indirect(offs_t[:]))
         x_picked.append(keep.tile([P, S], I32, name="x_picked1", tag="scales_then_codes", align_bytes=64))
         pick_x(1, 0)
         pick_x(1, 1)
-        quantize_w(0, 1, "vector")
-        quantize_w(1, 0, "vector")
-        step_exp(0)
-        old_first = keep.tile([P, S], F32, name="old_first")
+        old_first = reused.tile([P, S], F32, name="old_first", offset=0, align_bytes=64)
         nc.vector.tensor_copy(old_first[:], states[0][:].indirect(slot_t[:]))
+        round_w(1, 0, grouped_at(4096), nc.vector.tensor_copy)
+        round_w(0, 1, grouped_at(6144), nc.vector.tensor_copy)
+        quantize_w(1, 0)
+        quantize_w(0, 1)
+        step_exp(0)
         step_log(0)
         for b in range(BLOCKS):
             enter(b, 0)
             step_decay(b)
             keep_old(b)
+            if 0 < b < BLOCKS - 1:
+                round_w(1, b + 1, grouped_in(f"decay{b % 2}"), nc.vector.tensor_copy)
             put(b, 0)
+            if b == 0:
+                round_w(1, 1, grouped_in("entered0"), nc.vector.tensor_copy)
             if b + 1 < BLOCKS:
-                quantize_w(1, b + 1, "vector")
+                quantize_w(1, b + 1)
                 step_exp(b + 1)
                 step_log(b + 1)
             if b + 2 < BLOCKS:
-                quantize_w(0, b + 2, "vector", tag="soft")
+                grouped = after_log.tile(grouped_shape, BF16, name="grouped_late", offset=2048, align_bytes=64)
+                round_w(0, b + 2, grouped, nc.vector.tensor_copy)
             enter(b, 1)
+            if b + 2 < BLOCKS:
+                quantize_w(0, b + 2)
             put(b, 1)
             nc.sync.dma_start(out_0[b * P : (b + 1) * P, :], states[b][:])
             if b > 0:

@@ -25,6 +25,12 @@ LIST_COLS = HALF // 16
 QUARTER = U // 4
 CLAMP = 32.0
 W_PIECES = ((0, 1), (1, 1), (2, 2))
+KIB = 1024
+X_TABLE_AT = (8 * KIB - 64, 36 * KIB - 64)
+STATE_AT = (0, 28 * KIB, 52 * KIB, 8 * KIB)
+W_AT = {(1, 0): 8 * KIB, (0, 1): 12 * KIB, (1, 1): 20 * KIB, (0, 2): 36 * KIB, (1, 2): 44 * KIB, (0, 0): 60 * KIB}
+PICKED_AT = 16 * KIB
+OLD_AT = 52 * KIB
 
 
 def tile_picked_ymamba_step_po_kernel(
@@ -41,17 +47,21 @@ def tile_picked_ymamba_step_po_kernel(
         offs_t = keep.tile([P, S // 16], U16, name="offs_t")
         slot_t = keep.tile([P, S // 16], U16, name="slot_t")
         x_table = [
-            keep.tile([P, T], I32, name="x_table0"),
-            reused.tile([P, T], I32, name="x_table1", offset=0, align_bytes=64),
+            reused.tile([P, T], I32, name=f"x_table{g}", offset=X_TABLE_AT[g], align_bytes=64) for g in range(PASSES)
         ]
         scale_table = keep.tile([P, T], U8, name="scale_table", tag="scales_then_codes", align_bytes=64)
-        x_picked = [keep.tile([P, S], I32, name="x_picked0", align_bytes=64)]
+        scale_picked = keep.tile([P, S], U8, name="scale_picked")
+        x_picked = [None, reused.tile([P, S], I32, name="x_picked1", offset=PICKED_AT, align_bytes=64)]
         x_plane = keep.tile([P, S], U8, name="x_plane", align_bytes=64)
-        states = [keep.tile([P, U], F32, name=f"states{b}") for b in range(BLOCKS)]
+        states = [
+            reused.tile([P, U], F32, name=f"states{b}", offset=STATE_AT[b], align_bytes=64) for b in range(BLOCKS)
+        ]
         w_raw = {}
         for i in range(2):
             for first, count in W_PIECES:
-                tile = keep.tile([P, PASSES, 4, count * P], F32, name=f"w_raw{i}_{first}")
+                tile = reused.tile(
+                    [P, PASSES, 4, count * P], F32, name=f"w_raw{i}_{first}", offset=W_AT[i, first], align_bytes=64
+                )
                 for b in range(first, first + count):
                     w_raw[i, b] = (tile, b - first)
         channel_rows = keep.tile([P, P], F32, name="channel_rows")
@@ -75,29 +85,19 @@ def tile_picked_ymamba_step_po_kernel(
         def load_state(b):
             nc.sync.dma_start(states[b][:], state[b * P : (b + 1) * P, :])
 
-        nc.vector.memset(channel_rows[:], 0.0)
-        nc.scalar.dma_start(channel_rows[0:BLOCKS, :], bias.rearrange("(b p) o -> b (p o)", p=P))
-        nc.scalar.dma_start(channel_rows[BLOCKS : 2 * BLOCKS, :], rate.rearrange("(b p) o -> b (p o)", p=P))
-        nc.gpsimd.memset(scale_table[:].bitcast(I32), 0)
-        for g in range(PASSES):
-            for r in range(4):
-                nc.gpsimd.dma_start(
-                    scale_table[4 * g + r : P : 32, :].bitcast(I32), x_scales[g, r:16:4, :].bitcast(I32)
-                )
+        nc.vector.memset(scale_table[:].bitcast(I32), 0)
+        nc.scalar.dma_start(
+            scale_table[0:P:4, :].bitcast(I32), x_scales.rearrange("g q n -> (g q) n").bitcast(I32)
+        )
+        nc.vector.memset(x_plane[:].bitcast(I32), 0)
+        nc.gpsimd.memset(channel_rows[:], 0.0)
+        nc.gpsimd.dma_start(channel_rows[0:BLOCKS, :], bias.rearrange("(b p) o -> b (p o)", p=P))
+        nc.gpsimd.dma_start(channel_rows[BLOCKS : 2 * BLOCKS, :], rate.rearrange("(b p) o -> b (p o)", p=P))
         nc.sync.dma_start(offs_t[:], offs)
         nc.sync.dma_start(slot_t[:], slot)
-        load_x(0)
         load_w(0, 0)
+        load_x(0)
         load_x(1)
-        load_state(0)
-        load_w(1, 0)
-        load_w(0, 1)
-        load_w(1, 1)
-        load_w(0, 2)
-        load_state(1)
-        load_w(1, 2)
-        load_state(2)
-        load_state(3)
         make_identity(nc, ident[:])
 
         channel_turned = psum.tile([P, P], F32, name="channel_turned", tag="turned")
@@ -117,9 +117,6 @@ def tile_picked_ymamba_step_po_kernel(
 
         def grouped_in(tag):
             return keep.tile(grouped_shape, BF16, name="grouped", tag=tag, align_bytes=64)
-
-        def grouped_at(offset):
-            return reused.tile(grouped_shape, BF16, name=f"grouped_at{offset}", offset=offset, align_bytes=64)
 
         def round_w(i, b, grouped, copy):
             tile, place = w_raw[i, b]
@@ -275,18 +272,34 @@ def tile_picked_ymamba_step_po_kernel(
                 )
             store_codes(b, codes, (nc.sync, nc.scalar))
 
+        nc.vector.tensor_copy(scale_picked[:], scale_table[:].indirect(offs_t[:]))
+        for g in range(PASSES):
+            for q in range(4):
+                queue = nc.gpsimd if 4 * g + q < 3 else nc.scalar
+                src = 64 * g + 16 * q
+                dst = 32 * q + 4 * g
+                queue.dma_start(
+                    x_plane[dst : dst + 4, :].bitcast(I32), scale_picked[src : src + 16 : 4, :].bitcast(I32)
+                )
+        x_picked[0] = keep.tile([P, S], I32, name="x_picked0", tag="scales_then_codes", align_bytes=64)
         pick_x(0, 0)
         pick_x(0, 1)
+        load_state(0)
+        load_w(1, 0)
+        load_w(0, 1)
+        load_w(1, 1)
         round_w(0, 0, grouped_in("grouped"), nc.scalar.copy)
         quantize_w(0, 0)
-        nc.vector.tensor_copy(x_plane[:], scale_table[:].indirect(offs_t[:]))
-        x_picked.append(keep.tile([P, S], I32, name="x_picked1", tag="scales_then_codes", align_bytes=64))
         pick_x(1, 0)
         pick_x(1, 1)
-        old_first = reused.tile([P, S], F32, name="old_first", offset=0, align_bytes=64)
+        load_w(0, 2)
+        load_state(1)
+        load_w(1, 2)
+        old_first = reused.tile([P, S], F32, name="old_first", offset=OLD_AT, align_bytes=64)
         nc.vector.tensor_copy(old_first[:], states[0][:].indirect(slot_t[:]))
-        round_w(1, 0, grouped_at(4096), nc.vector.tensor_copy)
-        round_w(0, 1, grouped_at(6144), nc.vector.tensor_copy)
+        round_w(1, 0, grouped_in("grouped"), nc.vector.tensor_copy)
+        round_w(0, 1, grouped_in("grouped_b"), nc.vector.tensor_copy)
+        load_state(3)
         quantize_w(1, 0)
         quantize_w(0, 1)
         step_exp(0)
@@ -295,6 +308,8 @@ def tile_picked_ymamba_step_po_kernel(
             enter(b, 0)
             step_decay(b)
             keep_old(b)
+            if b == 0:
+                load_state(2)
             if 0 < b < BLOCKS - 1:
                 round_w(1, b + 1, grouped_in(f"decay{b % 2}"), nc.vector.tensor_copy)
             put(b, 0)

@@ -120,12 +120,14 @@ def tile_picked_ymamba_step_po_kernel(
 
         def round_w(i, b, grouped, copy):
             tile, place = w_raw[i, b]
-            copy(grouped[:], tile[:, :, :, place * P : (place + 1) * P].rearrange("p g j c -> p g c j"))
+            raw = tile[:, :, :, place * P : (place + 1) * P]
+            copy(grouped[:].rearrange("p g (c i) j -> p g c j i", i=4), raw.rearrange("p g j (c i) -> p g c j i", i=4))
             w_rounded[i, b] = grouped
 
-        def quantize_w(i, b):
+        def quantize_w(i, b, codes=None):
             grouped = w_rounded[i, b]
-            codes = keep.tile([P, PASSES * P], I32, name=f"w_codes{i}_{b}", align_bytes=64)
+            if codes is None:
+                codes = keep.tile([P, PASSES * P], I32, name=f"w_codes{i}_{b}", align_bytes=64)
             plane = keep.tile([P, PASSES * P], U8, name=f"w_plane{i}_{b}", align_bytes=64)
             nc.vector.quantize_mx(codes[:].bitcast(FP8X4), plane[:], grouped[:].rearrange("p g c j -> p (g c j)"))
             w_codes[i, b] = (codes, plane)
@@ -150,15 +152,17 @@ def tile_picked_ymamba_step_po_kernel(
 
         def step_exp(b):
             below = work.tile([P, S], F32, name="below")
+            grown = keep.tile([P, S], F32, name="grown", tag="grown")
             zs = []
             for h in range(HALVES):
+                cols = slice(h * HALF, (h + 1) * HALF)
                 z = product(0, b, h, "z")
-                nc.scalar.activation(
-                    below[:, h * HALF : (h + 1) * HALF], z[:], ACT.Relu, bias=room_t[:, b : b + 1], scale=-1.0
-                )
+                nc.scalar.activation(below[:, cols], z[:], ACT.Relu, bias=room_t[:, b : b + 1], scale=-1.0)
+                if b == 0:
+                    nc.scalar.activation(grown[:, cols], below[:, cols], ACT.Exp, bias=CLAMP, scale=-1.0)
                 zs.append(z)
-            grown = keep.tile([P, S], F32, name="grown", tag="grown")
-            nc.scalar.activation(grown[:], below[:], ACT.Exp, bias=CLAMP, scale=-1.0)
+            if b > 0:
+                nc.scalar.activation(grown[:], below[:], ACT.Exp, bias=CLAMP, scale=-1.0)
             held[b] = (grown, zs)
 
         dts = {}
@@ -170,12 +174,9 @@ def tile_picked_ymamba_step_po_kernel(
             grown, zs = held[b]
             dt = work.tile([P, S], F32, name="dt")
             soft = after_log.tile([P, S], F32, name="soft", offset=0, align_bytes=64)
-            if b > 0:
-                nc.scalar.activation(soft[:], grown[:], ACT.Ln, bias=1.0)
+            nc.scalar.activation(soft[:], grown[:], ACT.Ln, bias=1.0)
             for h in range(HALVES):
                 cols = slice(h * HALF, (h + 1) * HALF)
-                if b == 0:
-                    nc.scalar.activation(soft[:, cols], grown[:, cols], ACT.Ln, bias=1.0)
                 nc.vector.scalar_tensor_tensor(
                     dt[:, cols], zs[h][:], bias_t[:, b : b + 1], soft[:, cols], ALU.add, ALU.max
                 )
@@ -199,19 +200,22 @@ def tile_picked_ymamba_step_po_kernel(
             entered[b, h] = tile
 
         def keep_old(b):
-            kept = work.tile([P, S], F32, name="kept")
             if b == 0:
                 for h in range(HALVES):
                     cols = slice(h * HALF, (h + 1) * HALF)
-                    nc.vector.tensor_tensor(kept[:, cols], old_first[:, cols], decays[b][:, cols], ALU.mult)
+                    kept = keep.tile([P, HALF], F32, name=f"kept_first{h}", align_bytes=64)
+                    nc.vector.tensor_tensor(kept[:], old_first[:, cols], decays[b][:, cols], ALU.mult)
+                    kepts[b, h] = kept[:]
             else:
+                kept = work.tile([P, S], F32, name="kept")
                 nc.vector.tensor_tensor(kept[:], states[b][:].indirect(slot_t[:]), decays[b][:], ALU.mult)
-            kepts[b] = kept
+                for h in range(HALVES):
+                    kepts[b, h] = kept[:, h * HALF : (h + 1) * HALF]
 
         def put(b, h):
             nc.vector.tensor_tensor(
                 states[b][:].indirect(slot_t[:, h * LIST_COLS : (h + 1) * LIST_COLS]),
-                kepts[b][:, h * HALF : (h + 1) * HALF],
+                kepts[b, h],
                 entered[b, h][:],
                 ALU.add,
             )
@@ -223,8 +227,8 @@ def tile_picked_ymamba_step_po_kernel(
                 nc.tensor.transpose(turned[:, h, :], states[b][:, c0 : c0 + P], ident[:])
             return turned[:].rearrange("p h (q u e) -> p u (h q) e", u=2, e=2)
 
-        def turn_back(rounded_pair):
-            back = psum.tile([P, 2, 2, P], F32, name="back")
+        def turn_back(rounded_pair, tag):
+            back = psum.tile([P, 2, 2, P], F32, name="back", tag=tag)
             for jj in range(2):
                 words = rounded_pair[jj].rearrange("p u w e -> p (u w e)").bitcast(F32)
                 for u in range(2):
@@ -236,19 +240,23 @@ def tile_picked_ymamba_step_po_kernel(
             for h in range(4):
                 queues[h % 2].dma_start(rows[:, h * QUARTER : (h + 1) * QUARTER], codes[32 * h : 32 * (h + 1), :])
 
-        def hand_on(b):
+        regroupeds = {}
+
+        def regroup(b):
             rounded = keep.tile([P, 4, 2, P, 2], BF16, name="rounded", tag="grown")
             for j in range(4):
-                nc.scalar.copy(rounded[:, j], turn(b, j, "turned"))
+                nc.scalar.copy(rounded[:, j], turn(b, j, "turned" if j < 2 else "turned_more"))
             regrouped = work.tile([P, 4, P, 2], F32, name="regrouped", align_bytes=64)
             for pair in range(2):
-                back = turn_back([rounded[:, 2 * pair], rounded[:, 2 * pair + 1]])
+                back = turn_back([rounded[:, 2 * pair], rounded[:, 2 * pair + 1]], "turned")
                 nc.scalar.copy(regrouped[:, 2 * pair : 2 * pair + 2, :, :], back)
-            codes = work.tile([P, QUARTER], I32, name="out_codes", align_bytes=64)
+            regroupeds[b] = regrouped
+
+        def hand_on(b, codes):
             nc.vector.quantize_mx(
                 codes[:].bitcast(FP8X4),
                 out_plane[4 * b : P, :],
-                regrouped[:].rearrange("p j c u -> p (j c u)").bitcast(BF16),
+                regroupeds[b][:].rearrange("p j c u -> p (j c u)").bitcast(BF16),
             )
             store_codes(b, codes, (nc.sync, nc.sync))
 
@@ -257,11 +265,11 @@ def tile_picked_ymamba_step_po_kernel(
             rounded = []
             for j in range(4):
                 piece = keep.tile([P, 2, P, 2], BF16, name=f"last_rounded{j}")
-                copies[j % 2](piece[:], turn(b, j, "turned" if j < 2 else "z"))
+                copies[j % 2](piece[:], turn(b, j, "turned" if j < 2 else "turned_more"))
                 rounded.append(piece[:])
-            codes = work.tile([P, QUARTER], I32, name="out_codes", align_bytes=64)
+            codes = keep.tile([P, QUARTER], I32, name="last_codes", align_bytes=64)
             for pair in range(2):
-                back = turn_back(rounded[2 * pair : 2 * pair + 2])
+                back = turn_back(rounded[2 * pair : 2 * pair + 2], "z")
                 regrouped = keep.tile([P, 2, P, 2], F32, name=f"last_regrouped{pair}", align_bytes=64)
                 copies[pair](regrouped[:], back)
                 cols = slice(pair * 2 * P, (pair + 1) * 2 * P)
@@ -293,8 +301,8 @@ def tile_picked_ymamba_step_po_kernel(
         pick_x(1, 0)
         pick_x(1, 1)
         load_w(0, 2)
-        load_state(1)
         load_w(1, 2)
+        load_state(1)
         old_first = reused.tile([P, S], F32, name="old_first", offset=OLD_AT, align_bytes=64)
         nc.vector.tensor_copy(old_first[:], states[0][:].indirect(slot_t[:]))
         round_w(1, 0, grouped_in("grouped"), nc.vector.tensor_copy)
@@ -304,31 +312,44 @@ def tile_picked_ymamba_step_po_kernel(
         quantize_w(0, 1)
         step_exp(0)
         step_log(0)
+
+        def after_step_size(shape, dtype, name):
+            return after_log.tile(shape, dtype, name=name, offset=2048, align_bytes=64)
+
         for b in range(BLOCKS):
             enter(b, 0)
+            if b == 0:
+                round_w(1, 1, after_step_size(grouped_shape, BF16, "grouped_early"), nc.vector.tensor_copy)
+                quantize_w(1, 1)
             step_decay(b)
             keep_old(b)
             if b == 0:
                 load_state(2)
-            if 0 < b < BLOCKS - 1:
-                round_w(1, b + 1, grouped_in(f"decay{b % 2}"), nc.vector.tensor_copy)
+            elif b == 1:
+                round_w(0, 3, grouped_in("decay1"), nc.vector.tensor_copy)
+            else:
+                hand_on(b - 2, keep.tile([P, QUARTER], I32, name="out_codes", tag=f"decay{b % 2}", align_bytes=64))
             put(b, 0)
             if b == 0:
-                round_w(1, 1, grouped_in("entered0"), nc.vector.tensor_copy)
+                round_w(0, 2, grouped_in("entered0"), nc.vector.tensor_copy)
+                round_w(1, 2, grouped_in("kept_first0"), nc.vector.tensor_copy)
+                quantize_w(0, 2)
+                quantize_w(1, 2)
             if b + 1 < BLOCKS:
-                quantize_w(1, b + 1)
                 step_exp(b + 1)
                 step_log(b + 1)
-            if b + 2 < BLOCKS:
-                grouped = after_log.tile(grouped_shape, BF16, name="grouped_late", offset=2048, align_bytes=64)
-                round_w(0, b + 2, grouped, nc.vector.tensor_copy)
+            if b == 2:
+                round_w(1, 3, after_step_size(grouped_shape, BF16, "grouped_late"), nc.vector.tensor_copy)
             enter(b, 1)
-            if b + 2 < BLOCKS:
-                quantize_w(0, b + 2)
+            if b == 1:
+                quantize_w(0, 3, after_step_size([P, PASSES * P], I32, "codes_late"))
+            if b == 2:
+                quantize_w(1, 3)
             put(b, 1)
             nc.sync.dma_start(out_0[b * P : (b + 1) * P, :], states[b][:])
             if b > 0:
-                hand_on(b - 1)
+                regroup(b - 1)
+        hand_on(BLOCKS - 2, after_log.tile([P, QUARTER], I32, name="codes_after", offset=0, align_bytes=64))
         hand_on_last(BLOCKS - 1)
         for h in range(4):
             (nc.scalar, nc.sync)[h % 2].dma_start(

@@ -17,7 +17,8 @@ ALU = mybir.AluOpType
 ACT = mybir.ActivationFunctionType
 
 P = 128
-PASSES = K // 512
+K_PASS = 512
+PASSES = K // K_PASS
 BLOCKS = N // P
 HALF = 512
 HALVES = S // HALF
@@ -25,12 +26,14 @@ LIST_COLS = HALF // 16
 QUARTER = U // 4
 CLAMP = 32.0
 W_PIECES = ((0, 1), (1, 1), (2, 2))
+
 KIB = 1024
 X_TABLE_AT = (8 * KIB - 64, 36 * KIB - 64)
 STATE_AT = (0, 28 * KIB, 52 * KIB, 8 * KIB)
-W_AT = {(1, 0): 8 * KIB, (0, 1): 12 * KIB, (1, 1): 20 * KIB, (0, 2): 36 * KIB, (1, 2): 44 * KIB, (0, 0): 60 * KIB}
+W_AT = {(1, 0): 8 * KIB, (0, 1): 12 * KIB, (1, 1): 20 * KIB, (0, 2): 36 * KIB, (1, 2): 44 * KIB, (0, 0): 36 * KIB}
 PICKED_AT = 16 * KIB
 OLD_AT = 52 * KIB
+UPPER_HALF_AT = 2 * KIB
 
 
 def tile_picked_ymamba_step_po_kernel(
@@ -79,7 +82,7 @@ def tile_picked_ymamba_step_po_kernel(
         def load_w(i, piece):
             first, count = W_PIECES[piece]
             for g in range(PASSES):
-                rows = weights[i][g * 512 : (g + 1) * 512, first * P : (first + count) * P]
+                rows = weights[i][g * K_PASS : (g + 1) * K_PASS, first * P : (first + count) * P]
                 nc.sync.dma_start(w_raw[i, first][0][:, g], rows.rearrange("(p j) c -> p j c", j=4))
 
         def load_state(b):
@@ -97,7 +100,6 @@ def tile_picked_ymamba_step_po_kernel(
         nc.sync.dma_start(slot_t[:], slot)
         load_w(0, 0)
         load_x(0)
-        load_x(1)
         make_identity(nc, ident[:])
 
         channel_turned = psum.tile([P, P], F32, name="channel_turned", tag="turned")
@@ -280,15 +282,18 @@ def tile_picked_ymamba_step_po_kernel(
                 )
             store_codes(b, codes, (nc.sync, nc.scalar))
 
+        round_w(0, 0, grouped_in("grouped"), nc.scalar.copy)
+        load_x(1)
         nc.vector.tensor_copy(scale_picked[:], scale_table[:].indirect(offs_t[:]))
         for g in range(PASSES):
             for q in range(4):
-                queue = nc.gpsimd if 4 * g + q < 3 else nc.scalar
+                queue = nc.gpsimd if (g, q) == (0, 0) else nc.scalar
                 src = 64 * g + 16 * q
                 dst = 32 * q + 4 * g
                 queue.dma_start(
                     x_plane[dst : dst + 4, :].bitcast(I32), scale_picked[src : src + 16 : 4, :].bitcast(I32)
                 )
+        quantize_w(0, 0)
         x_picked[0] = keep.tile([P, S], I32, name="x_picked0", tag="scales_then_codes", align_bytes=64)
         pick_x(0, 0)
         pick_x(0, 1)
@@ -296,8 +301,6 @@ def tile_picked_ymamba_step_po_kernel(
         load_w(1, 0)
         load_w(0, 1)
         load_w(1, 1)
-        round_w(0, 0, grouped_in("grouped"), nc.scalar.copy)
-        quantize_w(0, 0)
         pick_x(1, 0)
         pick_x(1, 1)
         load_w(0, 2)
@@ -314,7 +317,7 @@ def tile_picked_ymamba_step_po_kernel(
         step_log(0)
 
         def after_step_size(shape, dtype, name):
-            return after_log.tile(shape, dtype, name=name, offset=2048, align_bytes=64)
+            return after_log.tile(shape, dtype, name=name, offset=UPPER_HALF_AT, align_bytes=64)
 
         for b in range(BLOCKS):
             enter(b, 0)
@@ -345,11 +348,13 @@ def tile_picked_ymamba_step_po_kernel(
                 quantize_w(0, 3, after_step_size([P, PASSES * P], I32, "codes_late"))
             if b == 2:
                 quantize_w(1, 3)
+            if b == 3:
+                regroup(2)
+                hand_on(2, keep.tile([P, QUARTER], I32, name="codes_after", tag="entered0", align_bytes=64))
             put(b, 1)
             nc.sync.dma_start(out_0[b * P : (b + 1) * P, :], states[b][:])
-            if b > 0:
+            if 0 < b < BLOCKS - 1:
                 regroup(b - 1)
-        hand_on(BLOCKS - 2, after_log.tile([P, QUARTER], I32, name="codes_after", offset=0, align_bytes=64))
         hand_on_last(BLOCKS - 1)
         for h in range(4):
             (nc.scalar, nc.sync)[h % 2].dma_start(

from contextlib import ExitStack

import concourse.mybir as mybir
from concourse.masks import make_identity

K, T, S, N, U = 1024, 4096, 1024, 512, 2048
FLOPS = 2 * 2 * K * S * N

F32 = mybir.dt.float32
BF16 = mybir.dt.bfloat16
I32 = mybir.dt.int32
U32 = mybir.dt.uint32
U16 = mybir.dt.uint16
U8 = mybir.dt.uint8
FP8X4 = mybir.dt.float8_e4m3fn_x4
ALU = mybir.AluOpType
ACT = mybir.ActivationFunctionType

P = 128
K_PASS = 512
PASSES = K // K_PASS
BLOCKS = N // P
HALF = 512
HALVES = S // HALF
LIST_COLS = HALF // 16
QUARTER = U // 4
CLAMP = 32.0
W_PIECES = ((0, 1), (1, 1), (2, 2))

KIB = 1024
X_TABLE_AT = (8 * KIB - 64, 36 * KIB - 64)
STATE_AT = (0, 28 * KIB, 52 * KIB, 8 * KIB)
W_AT = {(1, 0): 8 * KIB, (0, 1): 12 * KIB, (1, 1): 20 * KIB, (0, 2): 36 * KIB, (1, 2): 44 * KIB, (0, 0): 36 * KIB}
PICKED_AT = 16 * KIB
OLD_AT = 52 * KIB
UPPER_HALF_AT = 2 * KIB


def tile_picked_ymamba_step_po_kernel(
    tc, x_words, x_scales, state, w1, w2, bias, rate, offs, slot, out_0, out_1, out_2
):
    nc = tc.nc
    with ExitStack() as ctx:
        keep = ctx.enter_context(tc.tile_pool(name="keep", bufs=1))
        reused = ctx.enter_context(tc.tile_pool(name="reused", bufs=1))
        after_log = ctx.enter_context(tc.tile_pool(name="after_log", bufs=1))
        work = ctx.enter_context(tc.tile_pool(name="work", bufs=2))
        psum = ctx.enter_context(tc.psum_pool(name="psum", bufs=2))

        offs_t = keep.tile([P, S // 16], U16, name="offs_t")
        slot_t = keep.tile([P, S // 16], U16, name="slot_t")
        x_table = [
            reused.tile([P, T], I32, name=f"x_table{g}", offset=X_TABLE_AT[g], align_bytes=64) for g in range(PASSES)
        ]
        scale_table = keep.tile([P, T], U8, name="scale_table", tag="scales_then_codes", align_bytes=64)
        scale_picked = keep.tile([P, S], U8, name="scale_picked")
        x_picked = [None, reused.tile([P, S], I32, name="x_picked1", offset=PICKED_AT, align_bytes=64)]
        x_plane = keep.tile([P, S], U8, name="x_plane", align_bytes=64)
        states = [
            reused.tile([P, U], F32, name=f"states{b}", offset=STATE_AT[b], align_bytes=64) for b in range(BLOCKS)
        ]
        w_raw = {}
        for i in range(2):
            for first, count in W_PIECES:
                tile = reused.tile(
                    [P, PASSES, 4, count * P], F32, name=f"w_raw{i}_{first}", offset=W_AT[i, first], align_bytes=64
                )
                for b in range(first, first + count):
                    w_raw[i, b] = (tile, b - first)
        channel_rows = keep.tile([P, P], F32, name="channel_rows")
        channel_cols = keep.tile([P, 2 * BLOCKS], F32, name="channel_cols")
        bias_t = channel_cols[:, 0:BLOCKS]
        rate_t = channel_cols[:, BLOCKS : 2 * BLOCKS]
        room_t = keep.tile([P, BLOCKS], F32, name="room_t")
        ident = keep.tile([P, P], F32, name="ident")
        out_plane = keep.tile([P, QUARTER], U8, name="out_plane", align_bytes=64)
        weights = (w1, w2)

        def load_x(g):
            nc.sync.dma_start(x_table[g][:], x_words[g].rearrange("p n t -> p (n t)").bitcast(I32))

        def load_w(i, piece):
            first, count = W_PIECES[piece]
            for g in range(PASSES):
                rows = weights[i][g * K_PASS : (g + 1) * K_PASS, first * P : (first + count) * P]
                nc.sync.dma_start(w_raw[i, first][0][:, g], rows.rearrange("(p j) c -> p j c", j=4))

        def load_state(b):
            nc.sync.dma_start(states[b][:], state[b * P : (b + 1) * P, :])

        nc.vector.memset(scale_table[:].bitcast(I32), 0)
        nc.scalar.dma_start(
            scale_table[0:P:4, :].bitcast(I32), x_scales.rearrange("g q n -> (g q) n").bitcast(I32)
        )
        nc.vector.memset(x_plane[:].bitcast(I32), 0)
        nc.gpsimd.memset(channel_rows[:], 0.0)
        nc.gpsimd.dma_start(channel_rows[0:BLOCKS, :], bias.rearrange("(b p) o -> b (p o)", p=P))
        nc.gpsimd.dma_start(channel_rows[BLOCKS : 2 * BLOCKS, :], rate.rearrange("(b p) o -> b (p o)", p=P))
        nc.sync.dma_start(offs_t[:], offs)
        nc.sync.dma_start(slot_t[:], slot)
        load_w(0, 0)
        load_x(0)
        make_identity(nc, ident[:])

        channel_turned = psum.tile([P, P], F32, name="channel_turned", tag="turned")
        nc.tensor.transpose(channel_turned[:], channel_rows[:], ident[:])
        nc.scalar.copy(channel_cols[:], channel_turned[:, 0 : 2 * BLOCKS])
        nc.scalar.activation(room_t[:], channel_turned[:, 0:BLOCKS], ACT.Copy, bias=CLAMP, scale=-1.0)

        def pick_x(g, h):
            nc.vector.tensor_copy(
                x_picked[g][:, h * HALF : (h + 1) * HALF].bitcast(U32),
                x_table[g][:].bitcast(U32).indirect(offs_t[:, h * LIST_COLS : (h + 1) * LIST_COLS]),
            )

        w_codes = {}
        w_rounded = {}
        grouped_shape = [P, PASSES, P, 4]

        def grouped_in(tag):
            return keep.tile(grouped_shape, BF16, name="grouped", tag=tag, align_bytes=64)

        def round_w(i, b, grouped, copy):
            tile, place = w_raw[i, b]
            raw = tile[:, :, :, place * P : (place + 1) * P]
            copy(grouped[:].rearrange("p g (c i) j -> p g c j i", i=4), raw.rearrange("p g j (c i) -> p g c j i", i=4))
            w_rounded[i, b] = grouped

        def quantize_w(i, b, codes=None):
            grouped = w_rounded[i, b]
            if codes is None:
                codes = keep.tile([P, PASSES * P], I32, name=f"w_codes{i}_{b}", align_bytes=64)
            plane = keep.tile([P, PASSES * P], U8, name=f"w_plane{i}_{b}", align_bytes=64)
            nc.vector.quantize_mx(codes[:].bitcast(FP8X4), plane[:], grouped[:].rearrange("p g c j -> p (g c j)"))
            w_codes[i, b] = (codes, plane)

        def product(i, b, h, name):
            codes, plane = w_codes[i, b]
            acc = psum.tile([P, HALF], F32, name=name)
            cols = slice(h * HALF, (h + 1) * HALF)
            for g in range(PASSES):
                nc.tensor.matmul_mx(
                    acc[:],
                    lhsT=codes[:, g * P : (g + 1) * P].bitcast(FP8X4),
                    lhsT_scale=plane[:, g * P : (g + 1) * P],
                    rhs=x_picked[g][:, cols].bitcast(FP8X4),
                    rhs_scale=x_plane[4 * g : P, cols],
                    start=(g == 0),
                    stop=(g == PASSES - 1),
                )
            return acc

        held = {}

        def step_exp(b):
            below = work.tile([P, S], F32, name="below")
            grown = keep.tile([P, S], F32, name="grown", tag="grown")
            zs = []
            for h in range(HALVES):
                cols = slice(h * HALF, (h + 1) * HALF)
                z = product(0, b, h, "z")
                nc.scalar.activation(below[:, cols], z[:], ACT.Relu, bias=room_t[:, b : b + 1], scale=-1.0)
                if b == 0:
                    nc.scalar.activation(grown[:, cols], below[:, cols], ACT.Exp, bias=CLAMP, scale=-1.0)
                zs.append(z)
            if b > 0:
                nc.scalar.activation(grown[:], below[:], ACT.Exp, bias=CLAMP, scale=-1.0)
            held[b] = (grown, zs)

        dts = {}
        decays = {}
        entered = {}
        kepts = {}

        def step_log(b):
            grown, zs = held[b]
            dt = work.tile([P, S], F32, name="dt")
            soft = after_log.tile([P, S], F32, name="soft", offset=0, align_bytes=64)
            nc.scalar.activation(soft[:], grown[:], ACT.Ln, bias=1.0)
            for h in range(HALVES):
                cols = slice(h * HALF, (h + 1) * HALF)
                nc.vector.scalar_tensor_tensor(
                    dt[:, cols], zs[h][:], bias_t[:, b : b + 1], soft[:, cols], ALU.add, ALU.max
                )
            dts[b] = dt

        def step_decay(b):
            decay = keep.tile([P, S], F32, name="decay", tag=f"decay{b % 2}", align_bytes=64)
            width = HALF if b == 0 else S
            for c0 in range(0, S, width):
                cols = slice(c0, c0 + width)
                nc.scalar.activation(decay[:, cols], dts[b][:, cols], ACT.Exp, scale=rate_t[:, b : b + 1])
            decays[b] = decay

        def enter(b, h):
            y = product(1, b, h, "y")
            if h == 0:
                tile = keep.tile([P, HALF], F32, name="entered0", align_bytes=64)
            else:
                tile = after_log.tile([P, HALF], F32, name="entered1", offset=0, align_bytes=64)
            nc.vector.tensor_tensor(tile[:], y[:], dts[b][:, h * HALF : (h + 1) * HALF], ALU.mult)
            entered[b, h] = tile

        def keep_old(b):
            if b == 0:
                for h in range(HALVES):
                    cols = slice(h * HALF, (h + 1) * HALF)
                    kept = keep.tile([P, HALF], F32, name=f"kept_first{h}", align_bytes=64)
                    nc.vector.tensor_tensor(kept[:], old_first[:, cols], decays[b][:, cols], ALU.mult)
                    kepts[b, h] = kept[:]
            else:
                kept = work.tile([P, S], F32, name="kept")
                nc.vector.tensor_tensor(kept[:], states[b][:].indirect(slot_t[:]), decays[b][:], ALU.mult)
                for h in range(HALVES):
                    kepts[b, h] = kept[:, h * HALF : (h + 1) * HALF]

        def put(b, h):
            nc.vector.tensor_tensor(
                states[b][:].indirect(slot_t[:, h * LIST_COLS : (h + 1) * LIST_COLS]),
                kepts[b, h],
                entered[b, h][:],
                ALU.add,
            )

        def turn(b, j, tag):
            turned = psum.tile([P, 4, P], F32, name="turned", tag=tag)
            for h in range(4):
                c0 = h * QUARTER + j * P
                nc.tensor.transpose(turned[:, h, :], states[b][:, c0 : c0 + P], ident[:])
            return turned[:].rearrange("p h (q u e) -> p u (h q) e", u=2, e=2)

        def turn_back(rounded_pair, tag):
            back = psum.tile([P, 2, 2, P], F32, name="back", tag=tag)
            for jj in range(2):
                words = rounded_pair[jj].rearrange("p u w e -> p (u w e)").bitcast(F32)
                for u in range(2):
                    nc.tensor.transpose(back[:, jj, u, :], words[:, u * P : (u + 1) * P], ident[:])
            return back[:].rearrange("p j u c -> p j c u")

        def store_codes(b, codes, queues):
            rows = out_1[0, 32 * b : 32 * (b + 1)].rearrange("q c r -> q (c r)").bitcast(I32)
            for h in range(4):
                queues[h % 2].dma_start(rows[:, h * QUARTER : (h + 1) * QUARTER], codes[32 * h : 32 * (h + 1), :])

        regroupeds = {}

        def regroup(b):
            rounded = keep.tile([P, 4, 2, P, 2], BF16, name="rounded", tag="grown")
            for j in range(4):
                nc.scalar.copy(rounded[:, j], turn(b, j, "turned" if j < 2 else "turned_more"))
            regrouped = work.tile([P, 4, P, 2], F32, name="regrouped", align_bytes=64)
            for pair in range(2):
                back = turn_back([rounded[:, 2 * pair], rounded[:, 2 * pair + 1]], "turned")
                nc.scalar.copy(regrouped[:, 2 * pair : 2 * pair + 2, :, :], back)
            regroupeds[b] = regrouped

        def hand_on(b, codes):
            nc.vector.quantize_mx(
                codes[:].bitcast(FP8X4),
                out_plane[4 * b : P, :],
                regroupeds[b][:].rearrange("p j c u -> p (j c u)").bitcast(BF16),
            )
            store_codes(b, codes, (nc.sync, nc.sync))

        def hand_on_last(b):
            copies = (nc.scalar.copy, nc.vector.tensor_copy)
            rounded = []
            for j in range(4):
                piece = keep.tile([P, 2, P, 2], BF16, name=f"last_rounded{j}")
                copies[j % 2](piece[:], turn(b, j, "turned" if j < 2 else "turned_more"))
                rounded.append(piece[:])
            codes = keep.tile([P, QUARTER], I32, name="last_codes", align_bytes=64)
            for pair in range(2):
                back = turn_back(rounded[2 * pair : 2 * pair + 2], "z")
                regrouped = keep.tile([P, 2, P, 2], F32, name=f"last_regrouped{pair}", align_bytes=64)
                copies[pair](regrouped[:], back)
                cols = slice(pair * 2 * P, (pair + 1) * 2 * P)
                nc.vector.quantize_mx(
                    codes[:, cols].bitcast(FP8X4),
                    out_plane[4 * b : P, cols],
                    regrouped[:].rearrange("p j c u -> p (j c u)").bitcast(BF16),
                )
            store_codes(b, codes, (nc.sync, nc.scalar))

        round_w(0, 0, grouped_in("grouped"), nc.scalar.copy)
        load_x(1)
        nc.vector.tensor_copy(scale_picked[:], scale_table[:].indirect(offs_t[:]))
        for g in range(PASSES):
            for q in range(4):
                queue = nc.gpsimd if (g, q) == (0, 0) else nc.scalar
                src = 64 * g + 16 * q
                dst = 32 * q + 4 * g
                queue.dma_start(
                    x_plane[dst : dst + 4, :].bitcast(I32), scale_picked[src : src + 16 : 4, :].bitcast(I32)
                )
        quantize_w(0, 0)
        x_picked[0] = keep.tile([P, S], I32, name="x_picked0", tag="scales_then_codes", align_bytes=64)
        pick_x(0, 0)
        pick_x(0, 1)
        load_state(0)
        load_w(1, 0)
        load_w(0, 1)
        load_w(1, 1)
        pick_x(1, 0)
        pick_x(1, 1)
        load_w(0, 2)
        load_w(1, 2)
        load_state(1)
        old_first = reused.tile([P, S], F32, name="old_first", offset=OLD_AT, align_bytes=64)
        nc.vector.tensor_copy(old_first[:], states[0][:].indirect(slot_t[:]))
        round_w(1, 0, grouped_in("grouped"), nc.vector.tensor_copy)
        round_w(0, 1, grouped_in("grouped_b"), nc.vector.tensor_copy)
        load_state(3)
        quantize_w(1, 0)
        quantize_w(0, 1)
        step_exp(0)
        step_log(0)

        def after_step_size(shape, dtype, name):
            return after_log.tile(shape, dtype, name=name, offset=UPPER_HALF_AT, align_bytes=64)

        for b in range(BLOCKS):
            enter(b, 0)
            if b == 0:
                round_w(1, 1, after_step_size(grouped_shape, BF16, "grouped_early"), nc.vector.tensor_copy)
                quantize_w(1, 1)
            step_decay(b)
            keep_old(b)
            if b == 0:
                load_state(2)
            elif b == 1:
                round_w(0, 3, grouped_in("decay1"), nc.vector.tensor_copy)
            else:
                hand_on(b - 2, keep.tile([P, QUARTER], I32, name="out_codes", tag=f"decay{b % 2}", align_bytes=64))
            put(b, 0)
            if b == 0:
                round_w(0, 2, grouped_in("entered0"), nc.vector.tensor_copy)
                round_w(1, 2, grouped_in("kept_first0"), nc.vector.tensor_copy)
                quantize_w(0, 2)
                quantize_w(1, 2)
            if b + 1 < BLOCKS:
                step_exp(b + 1)
                step_log(b + 1)
            if b == 2:
                round_w(1, 3, after_step_size(grouped_shape, BF16, "grouped_late"), nc.vector.tensor_copy)
            enter(b, 1)
            if b == 1:
                quantize_w(0, 3, after_step_size([P, PASSES * P], I32, "codes_late"))
            if b == 2:
                quantize_w(1, 3)
            if b == 3:
                regroup(2)
                hand_on(2, keep.tile([P, QUARTER], I32, name="codes_after", tag="entered0", align_bytes=64))
            put(b, 1)
            nc.sync.dma_start(out_0[b * P : (b + 1) * P, :], states[b][:])
            if 0 < b < BLOCKS - 1:
                regroup(b - 1)
        hand_on_last(BLOCKS - 1)
        for h in range(4):
            (nc.scalar, nc.sync)[h % 2].dma_start(
                out_2[0, :, h * QUARTER : (h + 1) * QUARTER].bitcast(I32),
                out_plane[32 * h : 32 * h + 16, :].bitcast(I32),
            )
